import numpy as np
import ml_dtypes


def mxq(x, axis, fmt="e4m3"):
    dtype, down = {"e4m3": (ml_dtypes.float8_e4m3fn, 7), "e5m2": (ml_dtypes.float8_e5m2, 14)}[fmt]
    v = np.moveaxis(np.asarray(x, np.float32).astype(ml_dtypes.bfloat16).astype(np.float64), axis, -1)
    blocks = v.reshape(v.shape[:-1] + (-1, 32))
    amax = np.abs(blocks).max(-1, keepdims=True)
    byte = np.maximum(np.where(amax > 0, np.frexp(amax)[1] - 1 + 127, 0) - down, 1)
    scale = np.exp2(byte - 127.0)
    codes = (blocks / scale).astype(np.float32).astype(dtype).astype(np.float64)
    return np.moveaxis((codes * scale).reshape(v.shape), -1, axis)


WIDE = False


def mx_kscale(k):
    if not WIDE:
        return np.ones(k)
    levels = np.array([10, -10, 5, -5, 0])
    if k % 512:
        return np.exp2(np.random.permutation(np.resize(levels, k // 32))).repeat(32)
    a = np.empty((k // 512, 16))
    for p in range(k // 512):
        a[p, :8] = np.random.permutation(np.resize(levels, 8))
        for g in range(8):
            far = levels[np.abs(levels - a[p, g]) >= 10]
            a[p, g + 8] = far[np.random.randint(len(far))]
    return np.exp2(a.ravel()).repeat(32)


def f64(x):
    return np.asarray(x).astype(np.float64)


def striped(idx):
    return np.tile(np.asarray(idx).reshape(-1, 16).T, (8, 1)).astype(np.uint16)


def unstriped(offs):
    return offs[:16].T.reshape(-1).astype(np.int64)


E2M1 = np.array([0.0, 0.5, 1.0, 1.5, 2.0, 3.0, 4.0, 6.0, -0.0, -0.5, -1.0, -1.5, -2.0, -3.0, -4.0, -6.0])


def pack_weight(w, fmt):
    k, n = w.shape
    w = f64(np.asarray(w, np.float32).astype(ml_dtypes.bfloat16)).reshape(k // 32, 32, n)
    amax = np.abs(w).max(1)
    if fmt == "e4m3":
        byte = np.frexp(amax)[1] - 1 + 127 - 7
    else:
        mant, ex = np.frexp(amax / 6.0)
        byte = np.where(mant > 0.5, ex, ex - 1) + 127
    byte = np.clip(np.where(amax > 0, byte, 1), 1, 254)
    scaled = (w * np.exp2(127.0 - byte)[:, None, :]).reshape(k, n).astype(np.float32)
    by_word = np.ascontiguousarray(scaled.reshape(k // 512, 128, 4, n).transpose(0, 1, 3, 2))
    if fmt == "e4m3":
        words = by_word.astype(ml_dtypes.float8_e4m3fn).view(np.uint8)
    else:
        c = by_word.astype(ml_dtypes.float4_e2m1fn).view(np.uint8) & 0xF
        words = (c[..., 0::2] | (c[..., 1::2] << 4)).reshape(k // 512, 128, 2 * n)
    return np.ascontiguousarray(words), np.ascontiguousarray(byte.astype(np.uint8).reshape(k // 512, 16, n))


def unpack_weight(words, scales, fmt):
    g, _, n = scales.shape
    words = np.ascontiguousarray(words).reshape(g, 128, n, -1)
    if fmt == "e4m3":
        vals = words.view(ml_dtypes.float8_e4m3fn).astype(np.float64)
    else:
        nib = np.empty((g, 128, n, 4), np.uint8)
        nib[..., 0::2] = words & 0xF
        nib[..., 1::2] = words >> 4
        vals = E2M1[nib]
    vals = vals * np.repeat(np.exp2(scales.astype(np.float64) - 127.0), 8, axis=1)[..., None]
    return vals.transpose(0, 1, 3, 2).reshape(g * 512, n)


B, N, T, D, NQ = 1, 512, 2048, 512, 256


def setup_inputs():
    n = np.random.standard_normal
    idx = np.random.permutation(T)[:B * N]
    s = mx_kscale(D)[:, None]
    mid = n((D, T))
    kp = pack_weight((mid + np.abs(n((D, T)))) / s, "e4m3")
    cp = pack_weight((mid - np.abs(n((D, T)))) / s, "e4m3")
    wp = pack_weight(mid / s, "e4m3")
    return {
        "qT": (n((B, D, NQ)) * s * (1.00 / np.sqrt(D))).astype(np.float32),
        "k_words": kp[0],
        "k_scales": kp[1],
        "c_words": cp[0],
        "c_scales": cp[1],
        "w_words": wp[0],
        "w_scales": wp[1],
        "offs": striped(idx),
    }


def reference(qT, k_words, k_scales, c_words, c_scales, w_words, w_scales, offs):
    idx = unstriped(offs)
    pick = lambda x, which: x[:, which].reshape(x.shape[0], B, -1).transpose(1, 0, 2)
    k = unpack_weight(k_words, k_scales, "e4m3")
    kg = pick(k, idx)
    c = unpack_weight(c_words, c_scales, "e4m3")
    cg = pick(c, idx)
    w = unpack_weight(w_words, w_scales, "e4m3")
    wg = pick(w, idx)
    qq = mxq(f64(qT), 1, "e4m3")
    hiq = mxq(np.maximum(f64(qT), 0.0), 1, "e4m3")
    loq = mxq(np.minimum(f64(qT), 0.0), 1, "e4m3")
    a = (hiq.transpose(0, 2, 1) @ kg) + (loq.transpose(0, 2, 1) @ cg)
    z = qq.transpose(0, 2, 1) @ wg
    y = a - z
    return y

@@ -1,0 +1,113 @@
+from contextlib import ExitStack
+
+import concourse.mybir as mybir
+
+F32 = mybir.dt.float32
+BF16 = mybir.dt.bfloat16
+I32 = mybir.dt.int32
+U32 = mybir.dt.uint32
+U16 = mybir.dt.uint16
+U8 = mybir.dt.uint8
+FP8X4 = mybir.dt.float8_e4m3fn_x4
+ALU = mybir.AluOpType
+ACT = mybir.ActivationFunctionType
+
+P = 128
+PACK = 4
+D = 512
+PAGES = 2048
+SLOTS = 512
+NQ = 256
+BLOCKS = 16
+HALF = SLOTS // 2
+PARK = P - BLOCKS
+
+FLOPS = 3 * 2 * NQ * SLOTS * D
+
+
+def tile_attend_questmid_topk_kernel(tc, qT, k_words, k_scales, c_words, c_scales, w_words, w_scales, offs, out):
+    nc = tc.nc
+    tables = (("w", w_words, w_scales), ("k", k_words, k_scales), ("c", c_words, c_scales))
+    with ExitStack() as ctx:
+        keep = ctx.enter_context(tc.tile_pool(name="keep", bufs=1))
+        psum = ctx.enter_context(tc.psum_pool(name="psum", bufs=1))
+
+        offsets = keep.tile([P, SLOTS // 16], U16, name="offsets")
+        nc.sync.dma_start(offsets[:], offs)
+
+        scale_rows = []
+        for name, words, scales in tables:
+            rows = keep.tile([P, PAGES], U8, name=name + "_scale_rows", align_bytes=64)
+            nc.sync.dma_start(rows[PARK:P, :].bitcast(I32), scales[0].bitcast(I32))
+            nc.vector.memset(rows[0:PARK, :].bitcast(I32), 0)
+            scale_rows.append(rows)
+            if name == "w":
+                q_raw = keep.tile([P, PACK, NQ], F32, name="q_raw")
+                nc.sync.dma_start(q_raw[:], qT[0].rearrange("(p j) w -> p j w", j=PACK))
+
+
+        word_tiles = []
+        for name, words, scales in tables:
+            wt = keep.tile([P, PAGES], I32, name=name + "_words", align_bytes=64)
+            nc.sync.dma_start(wt[:], words[0].rearrange("p n t -> p (n t)").bitcast(I32))
+            word_tiles.append(wt)
+
+        planes = keep.tile([P, 3 * SLOTS], U8, name="planes", align_bytes=64)
+        nc.vector.memset(planes[:].bitcast(I32), 0)
+
+        picked_rows = keep.tile([P, 3 * SLOTS], U8, name="picked_rows", align_bytes=64)
+        for t in range(3):
+            nc.vector.tensor_copy(picked_rows[:, t * SLOTS:(t + 1) * SLOTS], scale_rows[t][:].indirect(offsets[:]))
+
+        q_neg = keep.tile([P, NQ * PACK], BF16, name="q_neg", align_bytes=64)
+        q_hi = keep.tile([P, NQ * PACK], BF16, name="q_hi", align_bytes=64)
+        q_lo = keep.tile([P, NQ * PACK], BF16, name="q_lo", align_bytes=64)
+        nc.scalar.activation(q_neg[:].rearrange("p (w j) -> p w j", j=PACK), q_raw[:].rearrange("p j w -> p w j"), ACT.Copy, scale=-1.0)
+        nc.scalar.activation(q_hi[:], q_neg[:], ACT.Relu, scale=-1.0)
+
+        for quad in range(4):
+            nc.scalar.dma_start(planes[32 * quad:32 * quad + 4, :].bitcast(I32),
+                                picked_rows[PARK + 4 * quad:PARK + 4 * quad + 4, :].bitcast(I32))
+
+        nc.vector.tensor_scalar(q_lo[:], q_neg[:], -1.0, 0.0, ALU.mult, ALU.min)
+        q_codes, q_scales = [], []
+        for name, part in (("neg", q_neg), ("hi", q_hi), ("lo", q_lo)):
+            codes = keep.tile([P, NQ], U32, name="codes_" + name, align_bytes=64)
+            plane = keep.tile([P, NQ], U8, name="plane_" + name, align_bytes=64)
+            nc.vector.quantize_mx(out=codes[:].bitcast(FP8X4), scales=plane[:], in_=part[:])
+            q_codes.append(codes)
+            q_scales.append(plane)
+
+        banks = [[psum.tile([P, HALF], F32, name="bank%d%d" % (h, m)) for m in range(2)] for h in range(2)]
+
+        def product(t, picked, h):
+            for m in range(2):
+                rows = slice(m * P, (m + 1) * P)
+                nc.tensor.matmul_mx(
+                    out=banks[h][m][:],
+                    lhsT=q_codes[t][:, rows].bitcast(FP8X4),
+                    lhsT_scale=q_scales[t][:, rows],
+                    rhs=picked.bitcast(FP8X4),
+                    rhs_scale=planes[:, t * SLOTS + h * HALF:t * SLOTS + (h + 1) * HALF],
+                    start=(t == 0),
+                    stop=(t == 2),
+                )
+
+        for t in range(2):
+            picked = keep.tile([P, SLOTS], U32, name="picked%d" % t, align_bytes=64)
+            nc.vector.tensor_copy(picked[:], word_tiles[t][:].bitcast(U32).indirect(offsets[:]))
+            for h in range(2):
+                product(t, picked[:, h * HALF:(h + 1) * HALF], h)
+
+        for h in range(2):
+            picked = keep.tile([P, HALF], U32, name="picked2%d" % h, align_bytes=64)
+            nc.vector.tensor_copy(picked[:], word_tiles[2][:].bitcast(U32).indirect(offsets[:, h * HALF // 16:(h + 1) * HALF // 16]))
+            product(2, picked[:], h)
+        for h in range(2):
+            for m in range(2):
+                res = keep.tile([P, HALF], F32, name="res%d%d" % (h, m))
+                if h == 1 and m == 1:
+                    nc.vector.tensor_copy(res[:], banks[h][m][:])
+                else:
+                    nc.scalar.copy(res[:], banks[h][m][:])
+                nc.sync.dma_start(out[0, m * P:(m + 1) * P, h * HALF:(h + 1) * HALF], res[:])

@@ -20,14 +20,12 @@ SLOTS = 512
 NQ = 256
 BLOCKS = 16
 HALF = SLOTS // 2
-PARK = P - BLOCKS
 
 FLOPS = 3 * 2 * NQ * SLOTS * D
 
 
 def tile_attend_questmid_topk_kernel(tc, qT, k_words, k_scales, c_words, c_scales, w_words, w_scales, offs, out):
     nc = tc.nc
-    tables = (("w", w_words, w_scales), ("k", k_words, k_scales), ("c", c_words, c_scales))
     with ExitStack() as ctx:
         keep = ctx.enter_context(tc.tile_pool(name="keep", bufs=1))
         psum = ctx.enter_context(tc.psum_pool(name="psum", bufs=1))
@@ -35,41 +33,53 @@ def tile_attend_questmid_topk_kernel(tc, qT, k_words, k_scales, c_words, c_scale
         offsets = keep.tile([P, SLOTS // 16], U16, name="offsets")
         nc.sync.dma_start(offsets[:], offs)
 
-        scale_rows = []
-        for name, words, scales in tables:
-            rows = keep.tile([P, PAGES], U8, name=name + "_scale_rows", align_bytes=64)
-            nc.sync.dma_start(rows[PARK:P, :].bitcast(I32), scales[0].bitcast(I32))
-            nc.vector.memset(rows[0:PARK, :].bitcast(I32), 0)
-            scale_rows.append(rows)
-            if name == "w":
-                q_raw = keep.tile([P, PACK, NQ], F32, name="q_raw")
-                nc.sync.dma_start(q_raw[:], qT[0].rearrange("(p j) w -> p j w", j=PACK))
+        def load_scale_rows(scales, first, name, tag):
+            rows = keep.tile([P, PAGES], U8, name=name, tag=tag, align_bytes=64)
+            nc.sync.dma_start(rows[first:first + BLOCKS, :].bitcast(I32), scales[0].bitcast(I32))
+            nc.vector.memset(rows[0:first, :].bitcast(I32), 0)
+            if first + BLOCKS < P:
+                nc.vector.memset(rows[first + BLOCKS:P, :].bitcast(I32), 0)
+            return rows
 
-
-        word_tiles = []
-        for name, words, scales in tables:
-            wt = keep.tile([P, PAGES], I32, name=name + "_words", align_bytes=64)
+        def load_words(words, name, tag):
+            wt = keep.tile([P, PAGES], I32, name=name, tag=tag, align_bytes=64)
             nc.sync.dma_start(wt[:], words[0].rearrange("p n t -> p (n t)").bitcast(I32))
-            word_tiles.append(wt)
+            return wt
+
+        def move_rows(dst, src, first):
+            for quad in range(4):
+                nc.sync.dma_start(dst[32 * quad:32 * quad + 4, :].bitcast(I32),
+                                  src[first + 4 * quad:first + 4 * quad + 4, :].bitcast(I32))
+
+        w_rows = load_scale_rows(w_scales, 112, "w_rows", "w_rows")
+        q_raw = keep.tile([P, PACK, NQ], F32, name="q_raw")
+        nc.sync.dma_start(q_raw[:], qT[0].rearrange("(p j) w -> p j w", j=PACK))
+        k_rows = load_scale_rows(k_scales, 112, "k_rows", "shared")
+        c_rows = load_scale_rows(c_scales, 48, "c_rows", "c_rows")
+        w_tile = load_words(w_words, "w_tile", "w_tile")
+        k_tile = load_words(k_words, "k_tile", "k_tile")
 
         planes = keep.tile([P, 3 * SLOTS], U8, name="planes", align_bytes=64)
-        nc.vector.memset(planes[:].bitcast(I32), 0)
+        nc.gpsimd.memset(planes[:].bitcast(I32), 0)
 
-        picked_rows = keep.tile([P, 3 * SLOTS], U8, name="picked_rows", align_bytes=64)
-        for t in range(3):
-            nc.vector.tensor_copy(picked_rows[:, t * SLOTS:(t + 1) * SLOTS], scale_rows[t][:].indirect(offsets[:]))
+        picked_wk = keep.tile([P, 2 * SLOTS], U8, name="picked_wk", align_bytes=64)
+        picked_c = keep.tile([P, SLOTS], U8, name="picked_c", align_bytes=64)
+        nc.vector.tensor_copy(picked_wk[:, 0:SLOTS], w_rows[:].indirect(offsets[:]))
+        nc.vector.tensor_copy(picked_wk[:, SLOTS:2 * SLOTS], k_rows[:].indirect(offsets[:]))
+        move_rows(planes[:, 0:2 * SLOTS], picked_wk, 112)
+        c_tile = load_words(c_words, "c_tile", "shared")
+        nc.vector.tensor_copy(picked_c[:], c_rows[:].indirect(offsets[:]))
+        move_rows(planes[:, 2 * SLOTS:3 * SLOTS], picked_c, 48)
+        word_tiles = [w_tile, k_tile, c_tile]
 
         q_neg = keep.tile([P, NQ * PACK], BF16, name="q_neg", align_bytes=64)
         q_hi = keep.tile([P, NQ * PACK], BF16, name="q_hi", align_bytes=64)
         q_lo = keep.tile([P, NQ * PACK], BF16, name="q_lo", align_bytes=64)
         nc.scalar.activation(q_neg[:].rearrange("p (w j) -> p w j", j=PACK), q_raw[:].rearrange("p j w -> p w j"), ACT.Copy, scale=-1.0)
         nc.scalar.activation(q_hi[:], q_neg[:], ACT.Relu, scale=-1.0)
-
-        for quad in range(4):
-            nc.scalar.dma_start(planes[32 * quad:32 * quad + 4, :].bitcast(I32),
-                                picked_rows[PARK + 4 * quad:PARK + 4 * quad + 4, :].bitcast(I32))
-
-        nc.vector.tensor_scalar(q_lo[:], q_neg[:], -1.0, 0.0, ALU.mult, ALU.min)
+        q_lo_neg = keep.tile([P, NQ * PACK], BF16, name="q_lo_neg", align_bytes=64)
+        nc.scalar.activation(q_lo_neg[:], q_neg[:], ACT.Relu)
+        nc.scalar.activation(q_lo[:], q_lo_neg[:], ACT.Copy, scale=-1.0)
         q_codes, q_scales = [], []
         for name, part in (("neg", q_neg), ("hi", q_hi), ("lo", q_lo)):
             codes = keep.tile([P, NQ], U32, name="codes_" + name, align_bytes=64)
@@ -106,8 +116,10 @@ def tile_attend_questmid_topk_kernel(tc, qT, k_words, k_scales, c_words, c_scale
         for h in range(2):
             for m in range(2):
                 res = keep.tile([P, HALF], F32, name="res%d%d" % (h, m))
+                dst = out[0, m * P:(m + 1) * P, h * HALF:(h + 1) * HALF]
                 if h == 1 and m == 1:
                     nc.vector.tensor_copy(res[:], banks[h][m][:])
+                    nc.sync.dma_start(dst, res[:])
                 else:
                     nc.scalar.copy(res[:], banks[h][m][:])
-                nc.sync.dma_start(out[0, m * P:(m + 1) * P, h * HALF:(h + 1) * HALF], res[:])
+                    (nc.scalar if h == 1 else nc.sync).dma_start(dst, res[:])

@@ -88,38 +88,45 @@ def tile_attend_questmid_topk_kernel(tc, qT, k_words, k_scales, c_words, c_scale
             q_codes.append(codes)
             q_scales.append(plane)
 
-        banks = [[psum.tile([P, HALF], F32, name="bank%d%d" % (h, m)) for m in range(2)] for h in range(2)]
+        spans = ((0, HALF), (HALF, P), (HALF + P, P))
+        banks = [[psum.tile([P, width], F32, name="bank%d_%d" % (first, m)) for m in range(2)] for first, width in spans]
 
-        def product(t, picked, h):
-            for m in range(2):
-                rows = slice(m * P, (m + 1) * P)
-                nc.tensor.matmul_mx(
-                    out=banks[h][m][:],
-                    lhsT=q_codes[t][:, rows].bitcast(FP8X4),
-                    lhsT_scale=q_scales[t][:, rows],
-                    rhs=picked.bitcast(FP8X4),
-                    rhs_scale=planes[:, t * SLOTS + h * HALF:t * SLOTS + (h + 1) * HALF],
-                    start=(t == 0),
-                    stop=(t == 2),
-                )
+        def product(t, picked, base, s, m):
+            first, width = spans[s]
+            rows = slice(m * P, (m + 1) * P)
+            nc.tensor.matmul_mx(
+                out=banks[s][m][:],
+                lhsT=q_codes[t][:, rows].bitcast(FP8X4),
+                lhsT_scale=q_scales[t][:, rows],
+                rhs=picked[:, first - base:first - base + width].bitcast(FP8X4),
+                rhs_scale=planes[:, t * SLOTS + first:t * SLOTS + first + width],
+                start=(t == 0),
+                stop=(t == 2),
+            )
 
         for t in range(2):
             picked = keep.tile([P, SLOTS], U32, name="picked%d" % t, align_bytes=64)
             nc.vector.tensor_copy(picked[:], word_tiles[t][:].bitcast(U32).indirect(offsets[:]))
-            for h in range(2):
-                product(t, picked[:, h * HALF:(h + 1) * HALF], h)
+            for m in range(2):
+                for s in range(3):
+                    product(t, picked, 0, s, m)
 
         for h in range(2):
             picked = keep.tile([P, HALF], U32, name="picked2%d" % h, align_bytes=64)
             nc.vector.tensor_copy(picked[:], word_tiles[2][:].bitcast(U32).indirect(offsets[:, h * HALF // 16:(h + 1) * HALF // 16]))
-            product(2, picked[:], h)
-        for h in range(2):
             for m in range(2):
-                res = keep.tile([P, HALF], F32, name="res%d%d" % (h, m))
-                dst = out[0, m * P:(m + 1) * P, h * HALF:(h + 1) * HALF]
-                if h == 1 and m == 1:
-                    nc.vector.tensor_copy(res[:], banks[h][m][:])
-                    nc.sync.dma_start(dst, res[:])
+                for s in ((0,), (1, 2))[h]:
+                    product(2, picked, h * HALF, s, m)
+        for m in range(2):
+            res = keep.tile([P, HALF], F32, name="res0%d" % m)
+            nc.scalar.copy(res[:], banks[0][m][:])
+            nc.sync.dma_start(out[0, m * P:(m + 1) * P, 0:HALF], res[:])
+        for m in range(2):
+            res = keep.tile([P, HALF], F32, name="res1%d" % m)
+            for s in (1, 2):
+                part = res[:, (s - 1) * P:s * P]
+                if m == 1:
+                    nc.scalar.copy(part, banks[s][m][:])
                 else:
-                    nc.scalar.copy(res[:], banks[h][m][:])
-                    (nc.scalar if h == 1 else nc.sync).dma_start(dst, res[:])
+                    nc.vector.tensor_copy(part, banks[s][m][:])
+            (nc.scalar if m == 1 else nc.sync).dma_start(out[0, m * P:(m + 1) * P, HALF:SLOTS], res[:])

from contextlib import ExitStack

import concourse.mybir as mybir

F32 = mybir.dt.float32
BF16 = mybir.dt.bfloat16
I32 = mybir.dt.int32
U32 = mybir.dt.uint32
U16 = mybir.dt.uint16
U8 = mybir.dt.uint8
FP8X4 = mybir.dt.float8_e4m3fn_x4
ALU = mybir.AluOpType
ACT = mybir.ActivationFunctionType

P = 128
PACK = 4
D = 512
PAGES = 2048
SLOTS = 512
NQ = 256
BLOCKS = 16
HALF = SLOTS // 2

FLOPS = 3 * 2 * NQ * SLOTS * D


def tile_attend_questmid_topk_kernel(tc, qT, k_words, k_scales, c_words, c_scales, w_words, w_scales, offs, out):
    nc = tc.nc
    with ExitStack() as ctx:
        keep = ctx.enter_context(tc.tile_pool(name="keep", bufs=1))
        psum = ctx.enter_context(tc.psum_pool(name="psum", bufs=1))

        offsets = keep.tile([P, SLOTS // 16], U16, name="offsets")
        nc.sync.dma_start(offsets[:], offs)

        def load_scale_rows(scales, first, name, tag):
            rows = keep.tile([P, PAGES], U8, name=name, tag=tag, align_bytes=64)
            nc.sync.dma_start(rows[first:first + BLOCKS, :].bitcast(I32), scales[0].bitcast(I32))
            nc.vector.memset(rows[0:first, :].bitcast(I32), 0)
            if first + BLOCKS < P:
                nc.vector.memset(rows[first + BLOCKS:P, :].bitcast(I32), 0)
            return rows

        def load_words(words, name, tag):
            wt = keep.tile([P, PAGES], I32, name=name, tag=tag, align_bytes=64)
            nc.sync.dma_start(wt[:], words[0].rearrange("p n t -> p (n t)").bitcast(I32))
            return wt

        def move_rows(dst, src, first):
            for quad in range(4):
                nc.sync.dma_start(dst[32 * quad:32 * quad + 4, :].bitcast(I32),
                                  src[first + 4 * quad:first + 4 * quad + 4, :].bitcast(I32))

        w_rows = load_scale_rows(w_scales, 112, "w_rows", "w_rows")
        q_raw = keep.tile([P, PACK, NQ], F32, name="q_raw")
        nc.sync.dma_start(q_raw[:], qT[0].rearrange("(p j) w -> p j w", j=PACK))
        k_rows = load_scale_rows(k_scales, 112, "k_rows", "shared")
        c_rows = load_scale_rows(c_scales, 48, "c_rows", "c_rows")
        w_tile = load_words(w_words, "w_tile", "w_tile")
        k_tile = load_words(k_words, "k_tile", "k_tile")

        planes = keep.tile([P, 3 * SLOTS], U8, name="planes", align_bytes=64)
        nc.gpsimd.memset(planes[:].bitcast(I32), 0)

        picked_wk = keep.tile([P, 2 * SLOTS], U8, name="picked_wk", align_bytes=64)
        picked_c = keep.tile([P, SLOTS], U8, name="picked_c", align_bytes=64)
        nc.vector.tensor_copy(picked_wk[:, 0:SLOTS], w_rows[:].indirect(offsets[:]))
        nc.vector.tensor_copy(picked_wk[:, SLOTS:2 * SLOTS], k_rows[:].indirect(offsets[:]))
        move_rows(planes[:, 0:2 * SLOTS], picked_wk, 112)
        c_tile = load_words(c_words, "c_tile", "shared")
        nc.vector.tensor_copy(picked_c[:], c_rows[:].indirect(offsets[:]))
        move_rows(planes[:, 2 * SLOTS:3 * SLOTS], picked_c, 48)
        word_tiles = [w_tile, k_tile, c_tile]

        q_neg = keep.tile([P, NQ * PACK], BF16, name="q_neg", align_bytes=64)
        q_hi = keep.tile([P, NQ * PACK], BF16, name="q_hi", align_bytes=64)
        q_lo = keep.tile([P, NQ * PACK], BF16, name="q_lo", align_bytes=64)
        nc.scalar.activation(q_neg[:].rearrange("p (w j) -> p w j", j=PACK), q_raw[:].rearrange("p j w -> p w j"), ACT.Copy, scale=-1.0)
        nc.scalar.activation(q_hi[:], q_neg[:], ACT.Relu, scale=-1.0)
        q_lo_neg = keep.tile([P, NQ * PACK], BF16, name="q_lo_neg", align_bytes=64)
        nc.scalar.activation(q_lo_neg[:], q_neg[:], ACT.Relu)
        nc.scalar.activation(q_lo[:], q_lo_neg[:], ACT.Copy, scale=-1.0)
        q_codes, q_scales = [], []
        for name, part in (("neg", q_neg), ("hi", q_hi), ("lo", q_lo)):
            codes = keep.tile([P, NQ], U32, name="codes_" + name, align_bytes=64)
            plane = keep.tile([P, NQ], U8, name="plane_" + name, align_bytes=64)
            nc.vector.quantize_mx(out=codes[:].bitcast(FP8X4), scales=plane[:], in_=part[:])
            q_codes.append(codes)
            q_scales.append(plane)

        spans = ((0, HALF), (HALF, P), (HALF + P, P))
        banks = [[psum.tile([P, width], F32, name="bank%d_%d" % (first, m)) for m in range(2)] for first, width in spans]

        def product(t, picked, base, s, m):
            first, width = spans[s]
            rows = slice(m * P, (m + 1) * P)
            nc.tensor.matmul_mx(
                out=banks[s][m][:],
                lhsT=q_codes[t][:, rows].bitcast(FP8X4),
                lhsT_scale=q_scales[t][:, rows],
                rhs=picked[:, first - base:first - base + width].bitcast(FP8X4),
                rhs_scale=planes[:, t * SLOTS + first:t * SLOTS + first + width],
                start=(t == 0),
                stop=(t == 2),
            )

        for t in range(2):
            picked = keep.tile([P, SLOTS], U32, name="picked%d" % t, align_bytes=64)
            nc.vector.tensor_copy(picked[:], word_tiles[t][:].bitcast(U32).indirect(offsets[:]))
            for m in range(2):
                for s in range(3):
                    product(t, picked, 0, s, m)

        for h in range(2):
            picked = keep.tile([P, HALF], U32, name="picked2%d" % h, align_bytes=64)
            nc.vector.tensor_copy(picked[:], word_tiles[2][:].bitcast(U32).indirect(offsets[:, h * HALF // 16:(h + 1) * HALF // 16]))
            for m in range(2):
                for s in ((0,), (1, 2))[h]:
                    product(2, picked, h * HALF, s, m)
        for m in range(2):
            res = keep.tile([P, HALF], F32, name="res0%d" % m)
            nc.scalar.copy(res[:], banks[0][m][:])
            nc.sync.dma_start(out[0, m * P:(m + 1) * P, 0:HALF], res[:])
        for m in range(2):
            res = keep.tile([P, HALF], F32, name="res1%d" % m)
            for s in (1, 2):
                part = res[:, (s - 1) * P:s * P]
                if m == 1:
                    nc.scalar.copy(part, banks[s][m][:])
                else:
                    nc.vector.tensor_copy(part, banks[s][m][:])
            (nc.scalar if m == 1 else nc.sync).dma_start(out[0, m * P:(m + 1) * P, HALF:SLOTS], res[:])
